import numpy as np
import ml_dtypes


def mxq(x, axis, fmt="e4m3"):
    dtype, down = {"e4m3": (ml_dtypes.float8_e4m3fn, 7), "e5m2": (ml_dtypes.float8_e5m2, 14)}[fmt]
    v = np.moveaxis(np.asarray(x, np.float32).astype(ml_dtypes.bfloat16).astype(np.float64), axis, -1)
    blocks = v.reshape(v.shape[:-1] + (-1, 32))
    amax = np.abs(blocks).max(-1, keepdims=True)
    byte = np.maximum(np.where(amax > 0, np.frexp(amax)[1] - 1 + 127, 0) - down, 1)
    scale = np.exp2(byte - 127.0)
    codes = (blocks / scale).astype(np.float32).astype(dtype).astype(np.float64)
    return np.moveaxis((codes * scale).reshape(v.shape), -1, axis)


WIDE = False


def mx_kscale(k):
    if not WIDE:
        return np.ones(k)
    levels = np.array([10, -10, 5, -5, 0])
    if k % 512:
        return np.exp2(np.random.permutation(np.resize(levels, k // 32))).repeat(32)
    a = np.empty((k // 512, 16))
    for p in range(k // 512):
        a[p, :8] = np.random.permutation(np.resize(levels, 8))
        for g in range(8):
            far = levels[np.abs(levels - a[p, g]) >= 10]
            a[p, g + 8] = far[np.random.randint(len(far))]
    return np.exp2(a.ravel()).repeat(32)


def f64(x):
    return np.asarray(x).astype(np.float64)


def striped(idx):
    return np.tile(idx.reshape(-1, 16).T, (8, 1)).astype(np.uint16)


def unstriped(offs):
    return offs[:16].T.reshape(-1).astype(np.int64)


E2M1 = np.array([0.0, 0.5, 1.0, 1.5, 2.0, 3.0, 4.0, 6.0, -0.0, -0.5, -1.0, -1.5, -2.0, -3.0, -4.0, -6.0])


def pack_weight(w, fmt):
    k, n = w.shape
    w = f64(np.asarray(w, np.float32).astype(ml_dtypes.bfloat16)).reshape(k // 32, 32, n)
    amax = np.abs(w).max(1)
    if fmt == "e4m3":
        byte = np.frexp(amax)[1] - 1 + 127 - 7
    else:
        mant, ex = np.frexp(amax / 6.0)
        byte = np.where(mant > 0.5, ex, ex - 1) + 127
    byte = np.clip(np.where(amax > 0, byte, 1), 1, 254)
    scaled = (w * np.exp2(127.0 - byte)[:, None, :]).reshape(k, n).astype(np.float32)
    by_word = np.ascontiguousarray(scaled.reshape(k // 512, 128, 4, n).transpose(0, 1, 3, 2))
    if fmt == "e4m3":
        words = by_word.astype(ml_dtypes.float8_e4m3fn).view(np.uint8)
    else:
        c = by_word.astype(ml_dtypes.float4_e2m1fn).view(np.uint8) & 0xF
        words = (c[..., 0::2] | (c[..., 1::2] << 4)).reshape(k // 512, 128, 2 * n)
    return np.ascontiguousarray(words), np.ascontiguousarray(byte.astype(np.uint8).reshape(k // 512, 16, n))


def unpack_weight(words, scales, fmt):
    g, _, n = scales.shape
    words = np.ascontiguousarray(words).reshape(g, 128, n, -1)
    if fmt == "e4m3":
        vals = words.view(ml_dtypes.float8_e4m3fn).astype(np.float64)
    else:
        nib = np.empty((g, 128, n, 4), np.uint8)
        nib[..., 0::2] = words & 0xF
        nib[..., 1::2] = words >> 4
        vals = E2M1[nib]
    vals = vals * np.repeat(np.exp2(scales.astype(np.float64) - 127.0), 8, axis=1)[..., None]
    return vals.transpose(0, 1, 3, 2).reshape(g * 512, n)


def gelu(v):
    return 0.5 * v * (1.0 + np.tanh(np.sqrt(2.0 / np.pi) * (v + 0.044715 * v**3)))


K, KA, KB, H, T, S, T3, S2, P = 1536, 512, 1024, 1024, 4096, 1024, 2048, 512, 512

def setup_inputs():
    n = np.random.standard_normal
    s = mx_kscale(K)[:, None]
    u = mx_kscale(H)[:, None]
    d = {}
    strength = np.exp(np.random.uniform(-1.2, 1.2, T))
    d["tab_words"], d["tab_scales"] = pack_weight(n((K, T)) * s * strength, "e4m3")
    d["offs"] = striped(np.random.permutation(T)[:S])
    d["tab2_words"], d["tab2_scales"] = pack_weight(n((H, T3)) / u / H ** 0.5, "e4m3")
    d["offs2"] = striped(np.random.permutation(T3)[:S2])
    d["pos1"] = striped(np.random.permutation(S)[:P])
    d["pos2"] = striped(np.random.permutation(S)[:P])
    d["w4_words"], d["w4_scales"] = pack_weight(3.0 * n((KA, H)) / s[:KA] / K ** 0.5, "e2m1")
    d["wb"] = (3.0 * n((KB, H)) / s[KA:] / K ** 0.5).astype(np.float32)
    d["gain"] = (np.random.uniform(0.15, 0.33, H) * u[:, 0]).astype(np.float32)
    d["defect"] = (0.3 * n(S2)).astype(np.float32)
    return d

def reference(tab_words, tab_scales, offs, tab2_words, tab2_scales, offs2, pos1, pos2, w4_words, w4_scales, wb, gain, defect):
    v = unpack_weight(tab_words, tab_scales, "e4m3")[:, unstriped(offs)]
    v2 = unpack_weight(tab2_words, tab2_scales, "e4m3")[:, unstriped(offs2)]
    w4 = unpack_weight(w4_words, w4_scales, "e2m1")
    wq = mxq(f64(wb), 0, "e4m3")
    x = w4.T @ v[:KA] + wq.T @ v[KA:]
    h = f64(gain)[:, None] * np.sqrt(1.0 + np.abs(x))
    hq = mxq(h, 0, "e4m3")
    e = v2.T @ hq
    entry = e[:, unstriped(pos1)]
    exit_ = e[:, unstriped(pos2)]
    return f64(defect)[:, None] - np.sin(entry) * exit_

@@ -1,0 +1,292 @@
+import math
+from contextlib import ExitStack
+
+import concourse.mybir as mybir
+
+F32 = mybir.dt.float32
+BF16 = mybir.dt.bfloat16
+I32 = mybir.dt.int32
+U32 = mybir.dt.uint32
+U16 = mybir.dt.uint16
+U8 = mybir.dt.uint8
+FP8X4 = mybir.dt.float8_e4m3fn_x4
+FP4X4 = mybir.dt.float4_e2m1fn_x4
+ACT = mybir.ActivationFunctionType
+ALU = mybir.AluOpType
+
+P = 128
+PACK = 4
+K_PASS = P * PACK
+K, H, T, S, T2, S2, PAIRS = 1536, 1024, 4096, 1024, 2048, 512, 512
+K_PASSES = K // K_PASS
+R_PASSES = H // K_PASS
+J = 128
+J_CHUNKS = S // J
+E_COLS = 256
+M_TILES = S2 // P
+HALF = 512
+
+FLOPS = 2 * K * H * S + 2 * H * S2 * S
+
+
+def load_scale_rows(queue, plane, scales):
+    passes = scales.shape[0]
+    for quadrant in range(4):
+        queue.dma_start(
+            out=plane[32 * quadrant : 32 * quadrant + 4 * passes, :].bitcast(I32),
+            in_=scales[:, 4 * quadrant : 4 * quadrant + 4, :].bitcast(I32),
+        )
+
+
+def tile_list_chip_defect_scores_kernel(
+    tc, tab_words, tab_scales, offs, tab2_words, tab2_scales, offs2, pos1, pos2, w4_words, w4_scales, wb, gain, defect, out
+):
+    nc = tc.nc
+    with ExitStack() as ctx:
+        keep = ctx.enter_context(tc.tile_pool(name="keep", bufs=1))
+        ring = ctx.enter_context(tc.tile_pool(name="ring", bufs=3))
+        psum = ctx.enter_context(tc.psum_pool(name="psum", bufs=8))
+
+        def kept(shape, dtype, name):
+            return keep.tile(shape, dtype, name=name, align_bytes=64)
+
+        v_scale_tab = kept([P, T], U8, "v_scale_tab")
+        w4_scale_raw = kept([P, H], U8, "w4_scale_raw")
+        v2_scale_tab = kept([P, T2], U8, "v2_scale_tab")
+        one = kept([P, 1], F32, "one")
+        warm = kept([P, 1], F32, "warm")
+        nc.vector.memset(v_scale_tab[:].bitcast(I32), 0)
+        nc.vector.memset(w4_scale_raw[:].bitcast(I32), 0)
+        nc.vector.memset(v2_scale_tab[:].bitcast(I32), 0)
+        nc.vector.memset(one[:], 1.0)
+        nc.scalar.activation(warm[:], one[:], ACT.Sqrt, bias=one[:])
+
+        v_tab = [kept([P, T], I32, f"v_tab{a}") for a in range(K_PASSES)]
+        v2_tab = [kept([P, T2], I32, f"v2_tab{b}") for b in range(R_PASSES)]
+        wb_raw = [[kept([P, PACK, K_PASS], F32, f"wb_raw{b}_{a}") for a in range(2)] for b in range(R_PASSES)]
+        w4_raw = kept([P, 2 * H], U8, "w4_raw")
+        idx = kept([P, S // 16], U16, "idx")
+        idx2 = kept([P, S2 // 16], U16, "idx2")
+        p1 = kept([P, PAIRS // 16], U16, "p1")
+        p2 = kept([P, PAIRS // 16], U16, "p2")
+        gain_sb = kept([P, R_PASSES, PACK], F32, "gain_sb")
+        defect_sb = kept([P, M_TILES], F32, "defect_sb")
+
+        def load_words(tile, words):
+            nc.sync.dma_start(out=tile[:], in_=words.rearrange("p t i -> p (t i)").bitcast(I32))
+
+        def load_wb(b, a):
+            rows = wb[a * K_PASS : (a + 1) * K_PASS, b * K_PASS : (b + 1) * K_PASS]
+            nc.sync.dma_start(out=wb_raw[b][a][:], in_=rows.rearrange("(p i) c -> p i c", i=PACK))
+
+        load_words(v_tab[0], tab_words[0])
+        nc.sync.dma_start(idx[:], offs)
+        nc.sync.dma_start(out=w4_raw[:].bitcast(I32), in_=w4_words[0].bitcast(I32))
+        load_wb(0, 0)
+        load_wb(0, 1)
+        load_words(v_tab[1], tab_words[1])
+        load_words(v_tab[2], tab_words[2])
+        nc.sync.dma_start(out=gain_sb[:], in_=gain.rearrange("(b p t) -> p b t", p=P, t=PACK))
+        load_wb(1, 0)
+        load_wb(1, 1)
+        nc.sync.dma_start(idx2[:], offs2)
+        load_scale_rows(nc.sync, v2_scale_tab, tab2_scales)
+        load_words(v2_tab[0], tab2_words[0])
+        load_words(v2_tab[1], tab2_words[1])
+        nc.sync.dma_start(p1[:], pos1)
+        nc.sync.dma_start(p2[:], pos2)
+        with nc.allow_non_contiguous_dma(reason="one value a partition"):
+            nc.sync.dma_start(out=defect_sb[:], in_=defect.rearrange("(t p) -> p t", p=P))
+
+        load_scale_rows(nc.gpsimd, v_scale_tab, tab_scales)
+        load_scale_rows(nc.gpsimd, w4_scale_raw, w4_scales)
+
+        v_codes = [[kept([P, HALF], U32, f"v_codes{a}_{u}") for u in range(2)] for a in range(K_PASSES)]
+        v_scales = kept([P, S], U8, "v_scales")
+
+        def gather_v(a):
+            for u in range(2):
+                cols = idx[:, u * HALF // 16 : (u + 1) * HALF // 16]
+                nc.vector.tensor_copy(v_codes[a][u][:], v_tab[a][:].bitcast(U32).indirect(cols))
+
+        w4_codes = kept([P, 2 * H], U8, "w4_codes")
+        w4_plane = kept([P, H], U8, "w4_plane")
+        wq_codes = [[kept([P, K_PASS], U32, f"wq_codes{b}_{a}") for a in range(2)] for b in range(R_PASSES)]
+        wq_plane = [[kept([P, K_PASS], U8, f"wq_plane{b}_{a}") for a in range(2)] for b in range(R_PASSES)]
+
+        def round_wb(b, a, engine):
+            grouped = ring.tile([P, PACK * K_PASS], BF16, name="wb_grouped", align_bytes=64, bufs=2)
+            dst = grouped[:].rearrange("p (t m i) -> p m t i", t=PACK, i=PACK)
+            src = wb_raw[b][a][:].rearrange("p i (m t) -> p m t i", t=PACK)
+            if engine == "scalar":
+                nc.scalar.copy(dst, src)
+            else:
+                nc.vector.tensor_copy(dst, src)
+            return grouped
+
+        def quantize_wb(b, a, grouped):
+            nc.vector.quantize_mx(out=wq_codes[b][a][:].bitcast(FP8X4), scales=wq_plane[b][a][:], in_=grouped[:])
+
+        gather_v(0)
+        nc.vector.tensor_copy(v_scales[:], v_scale_tab[:].indirect(idx[:]))
+        for b in range(R_PASSES):
+            nc.vector.tensor_copy(
+                w4_codes[:, b * 2 * K_PASS : (b + 1) * 2 * K_PASS].rearrange("p (t m e) -> p t m e", t=PACK, e=2),
+                w4_raw[:, b * 2 * K_PASS : (b + 1) * 2 * K_PASS].rearrange("p (m t e) -> p t m e", t=PACK, e=2),
+            )
+        nc.vector.tensor_copy(
+            w4_plane[:].rearrange("p (b t m) -> p b t m", b=R_PASSES, t=PACK),
+            w4_scale_raw[:].rearrange("p (b m t) -> p b t m", b=R_PASSES, t=PACK),
+        )
+        g0 = round_wb(0, 0, "scalar")
+        g1 = round_wb(0, 1, "scalar")
+        quantize_wb(0, 0, g0)
+        gather_v(1)
+        quantize_wb(0, 1, g1)
+        gather_v(2)
+
+        def x_pass(bank, b, c, a):
+            u, col = divmod(c * J, HALF)
+            for t in range(PACK):
+                m0 = t * P
+                if a == 0:
+                    w0 = b * K_PASS + m0
+                    lhs = w4_codes[:, 2 * w0 : 2 * (w0 + P)].bitcast(FP4X4)
+                    lhs_scale = w4_plane[:, w0 : w0 + P]
+                else:
+                    lhs = wq_codes[b][a - 1][:, m0 : m0 + P].bitcast(FP8X4)
+                    lhs_scale = wq_plane[b][a - 1][:, m0 : m0 + P]
+                nc.tensor.matmul_mx(
+                    out=bank[:, t * J : (t + 1) * J],
+                    lhsT=lhs,
+                    lhsT_scale=lhs_scale,
+                    rhs=v_codes[a][u][:, col : col + J].bitcast(FP8X4),
+                    rhs_scale=v_scales[4 * a :, c * J : (c + 1) * J],
+                    start=(a == 0 and t == 0),
+                    stop=(a == K_PASSES - 1 and t == PACK - 1),
+                )
+
+        def new_bank():
+            return psum.tile([P, PACK * J], F32, name="bank")
+
+        e_chunks = S // E_COLS
+        h_codes = [[kept([P, E_COLS], U32, f"h_codes{b}_{q}") for q in range(e_chunks)] for b in range(R_PASSES)]
+        h_plane = [[kept([P, E_COLS], U8, f"h_plane{b}_{q}") for q in range(e_chunks)] for b in range(R_PASSES)]
+
+        def make_h(bank, b):
+            magnitude = ring.tile([P, J, PACK], F32, name="magnitude")
+            nc.scalar.activation(magnitude[:], bank[:].rearrange("p (t j) -> p j t", t=PACK), ACT.Abs)
+            root = ring.tile([P, J, PACK], F32, name="root")
+            nc.scalar.activation(root[:], magnitude[:], ACT.Sqrt, bias=one[:])
+            h_bf = ring.tile([P, J, PACK], BF16, name="h_bf", align_bytes=64)
+            nc.vector.tensor_tensor(h_bf[:], root[:], gain_sb[:, b : b + 1, :].broadcast_to([P, J, PACK]), ALU.mult)
+            return h_bf
+
+        def quantize_h(b, c, h_bf):
+            q, col = divmod(c * J, E_COLS)
+            nc.vector.quantize_mx(
+                out=h_codes[b][q][:, col : col + J].bitcast(FP8X4),
+                scales=h_plane[b][q][:, col : col + J],
+                in_=h_bf[:].rearrange("p j t -> p (j t)"),
+            )
+
+        v2_codes = [kept([P, S2], U32, f"v2_codes{b}") for b in range(R_PASSES)]
+        v2_scales = kept([P, S2], U8, "v2_scales")
+        scores = [kept([P, S], F32, f"scores{m}") for m in range(M_TILES)]
+
+        def make_scores(q):
+            for pair in range(M_TILES // 2):
+                bank = new_bank()
+                for b in range(R_PASSES):
+                    for s in range(2):
+                        m0 = (2 * pair + s) * P
+                        nc.tensor.matmul_mx(
+                            out=bank[:, s * E_COLS : (s + 1) * E_COLS],
+                            lhsT=v2_codes[b][:, m0 : m0 + P].bitcast(FP8X4),
+                            lhsT_scale=v2_scales[4 * b :, m0 : m0 + P],
+                            rhs=h_codes[b][q][:].bitcast(FP8X4),
+                            rhs_scale=h_plane[b][q][:],
+                            start=(b == 0 and s == 0),
+                            stop=(b == R_PASSES - 1 and s == 1),
+                        )
+                for s in range(2):
+                    dst = scores[2 * pair + s][:, q * E_COLS : (q + 1) * E_COLS]
+                    src = bank[:, s * E_COLS : (s + 1) * E_COLS]
+                    if pair == 0:
+                        nc.vector.tensor_copy(dst, src)
+                    else:
+                        nc.scalar.copy(dst, src)
+
+        banks = [new_bank() for c in range(J_CHUNKS)]
+        for a in range(K_PASSES - 1):
+            for c in range(J_CHUNKS):
+                x_pass(banks[c], 0, c, a)
+
+        pending = None
+        grouped1 = {}
+        for step in range(R_PASSES * J_CHUNKS):
+            b, c = divmod(step, J_CHUNKS)
+            if b == 0:
+                bank = banks[c]
+                x_pass(bank, b, c, K_PASSES - 1)
+            else:
+                bank = new_bank()
+                for a in range(K_PASSES):
+                    x_pass(bank, b, c, a)
+            h_bf = make_h(bank, b)
+            if pending is not None:
+                quantize_h(*pending)
+                pb, pc = pending[0], pending[1]
+                if pb == 1 and pc % 2 == 1:
+                    make_scores(pc // 2)
+            pending = (b, c, h_bf)
+            if step == 1:
+                grouped1[0] = round_wb(1, 0, "vector")
+            if step == 2:
+                quantize_wb(1, 0, grouped1[0])
+            if step == 3:
+                grouped1[1] = round_wb(1, 1, "vector")
+            if step == 4:
+                quantize_wb(1, 1, grouped1[1])
+            if step == 6:
+                nc.vector.tensor_copy(v2_scales[:], v2_scale_tab[:].indirect(idx2[:]))
+            if step == 7:
+                nc.vector.tensor_copy(v2_codes[0][:], v2_tab[0][:].bitcast(U32).indirect(idx2[:]))
+            if step == 8:
+                nc.vector.tensor_copy(v2_codes[1][:], v2_tab[1][:].bitcast(U32).indirect(idx2[:]))
+        quantize_h(*pending)
+        make_scores(e_chunks - 1)
+
+        entry = [kept([P, PAIRS], F32, f"entry{m}") for m in range(M_TILES)]
+        sines = {}
+
+        def pick_entry(m):
+            nc.vector.tensor_copy(entry[m][:], scores[m][:].indirect(p1[:]))
+
+        def count_turns(m):
+            turns = ring.tile([P, PAIRS], I32, name="turns", bufs=2)
+            nc.vector.tensor_scalar(turns[:], entry[m][:], 1.0 / (2.0 * math.pi), None, ALU.mult)
+            return turns
+
+        def sine(m, turns):
+            angle = ring.tile([P, PAIRS], F32, name="angle", bufs=2)
+            nc.vector.scalar_tensor_tensor(angle[:], turns[:], -2.0 * math.pi, entry[m][:], ALU.mult, ALU.add)
+            sines[m] = ring.tile([P, PAIRS], F32, name="sine")
+            nc.scalar.activation(sines[m][:], angle[:], ACT.Sin)
+
+        def finish(m):
+            product = ring.tile([P, PAIRS], F32, name="product", bufs=2)
+            nc.vector.tensor_tensor(product[:], scores[m][:].indirect(p2[:]), sines[m][:], ALU.mult)
+            result = ring.tile([P, PAIRS], F32, name="result", bufs=2)
+            nc.scalar.activation(result[:], product[:], ACT.Identity, bias=defect_sb[:, m : m + 1], scale=-1.0)
+            nc.sync.dma_start(out=out[m * P : (m + 1) * P, :], in_=result[:])
+
+        pick_entry(0)
+        for m in range(M_TILES):
+            if m + 1 < M_TILES:
+                pick_entry(m + 1)
+            turns = count_turns(m)
+            if m > 0:
+                finish(m - 1)
+            sine(m, turns)
+        finish(M_TILES - 1)

@@ -79,27 +79,27 @@ def tile_list_chip_defect_scores_kernel(
             rows = wb[a * K_PASS : (a + 1) * K_PASS, b * K_PASS : (b + 1) * K_PASS]
             nc.sync.dma_start(out=wb_raw[b][a][:], in_=rows.rearrange("(p i) c -> p i c", i=PACK))
 
-        load_words(v_tab[0], tab_words[0])
+        load_scale_rows(nc.scalar, v_scale_tab, tab_scales)
+        load_scale_rows(nc.scalar, w4_scale_raw, w4_scales)
+        load_scale_rows(nc.gpsimd, v2_scale_tab, tab2_scales)
         nc.sync.dma_start(idx[:], offs)
+        nc.sync.dma_start(out=gain_sb[:], in_=gain.rearrange("(b p t) -> p b t", p=P, t=PACK))
+        nc.sync.dma_start(idx2[:], offs2)
+        nc.sync.dma_start(p1[:], pos1)
+        nc.sync.dma_start(p2[:], pos2)
+        load_words(v_tab[0], tab_words[0])
         nc.sync.dma_start(out=w4_raw[:].bitcast(I32), in_=w4_words[0].bitcast(I32))
         load_wb(0, 0)
         load_wb(0, 1)
         load_words(v_tab[1], tab_words[1])
         load_words(v_tab[2], tab_words[2])
-        nc.sync.dma_start(out=gain_sb[:], in_=gain.rearrange("(b p t) -> p b t", p=P, t=PACK))
         load_wb(1, 0)
         load_wb(1, 1)
-        nc.sync.dma_start(idx2[:], offs2)
-        load_scale_rows(nc.sync, v2_scale_tab, tab2_scales)
         load_words(v2_tab[0], tab2_words[0])
         load_words(v2_tab[1], tab2_words[1])
-        nc.sync.dma_start(p1[:], pos1)
-        nc.sync.dma_start(p2[:], pos2)
         with nc.allow_non_contiguous_dma(reason="one value a partition"):
             nc.sync.dma_start(out=defect_sb[:], in_=defect.rearrange("(t p) -> p t", p=P))
 
-        load_scale_rows(nc.gpsimd, v_scale_tab, tab_scales)
-        load_scale_rows(nc.gpsimd, w4_scale_raw, w4_scales)
 
         v_codes = [[kept([P, HALF], U32, f"v_codes{a}_{u}") for u in range(2)] for a in range(K_PASSES)]
         v_scales = kept([P, S], U8, "v_scales")
@@ -143,6 +143,8 @@ def tile_list_chip_defect_scores_kernel(
         quantize_wb(0, 0, g0)
         gather_v(1)
         quantize_wb(0, 1, g1)
+        v2_scales = kept([P, S2], U8, "v2_scales")
+        nc.vector.tensor_copy(v2_scales[:], v2_scale_tab[:].indirect(idx2[:]))
         gather_v(2)
 
         def x_pass(bank, b, c, a):
@@ -173,25 +175,29 @@ def tile_list_chip_defect_scores_kernel(
         h_codes = [[kept([P, E_COLS], U32, f"h_codes{b}_{q}") for q in range(e_chunks)] for b in range(R_PASSES)]
         h_plane = [[kept([P, E_COLS], U8, f"h_plane{b}_{q}") for q in range(e_chunks)] for b in range(R_PASSES)]
 
-        def make_h(bank, b):
-            magnitude = ring.tile([P, J, PACK], F32, name="magnitude")
-            nc.scalar.activation(magnitude[:], bank[:].rearrange("p (t j) -> p j t", t=PACK), ACT.Abs)
-            root = ring.tile([P, J, PACK], F32, name="root")
-            nc.scalar.activation(root[:], magnitude[:], ACT.Sqrt, bias=one[:])
-            h_bf = ring.tile([P, J, PACK], BF16, name="h_bf", align_bytes=64)
-            nc.vector.tensor_tensor(h_bf[:], root[:], gain_sb[:, b : b + 1, :].broadcast_to([P, J, PACK]), ALU.mult)
+        def take_abs(bank, magnitude):
+            nc.scalar.activation(magnitude, bank[:].rearrange("p (t j) -> p j t", t=PACK), ACT.Abs)
+
+        def take_root(magnitude, width):
+            root = ring.tile([P, E_COLS, PACK], F32, name="root")
+            nc.scalar.activation(root[:, :width, :], magnitude[:, :width, :], ACT.Sqrt, bias=one[:])
+            return root
+
+        def apply_gain(root, b, width):
+            h_bf = ring.tile([P, E_COLS, PACK], BF16, name="h_bf", align_bytes=64, bufs=2)
+            gains = gain_sb[:, b : b + 1, :].broadcast_to([P, width, PACK])
+            nc.vector.tensor_tensor(h_bf[:, :width, :], root[:, :width, :], gains, ALU.mult)
             return h_bf
 
-        def quantize_h(b, c, h_bf):
+        def quantize_h(b, c, width, h_bf):
             q, col = divmod(c * J, E_COLS)
             nc.vector.quantize_mx(
-                out=h_codes[b][q][:, col : col + J].bitcast(FP8X4),
-                scales=h_plane[b][q][:, col : col + J],
-                in_=h_bf[:].rearrange("p j t -> p (j t)"),
+                out=h_codes[b][q][:, col : col + width].bitcast(FP8X4),
+                scales=h_plane[b][q][:, col : col + width],
+                in_=h_bf[:, :width, :].rearrange("p j t -> p (j t)"),
             )
 
         v2_codes = [kept([P, S2], U32, f"v2_codes{b}") for b in range(R_PASSES)]
-        v2_scales = kept([P, S2], U8, "v2_scales")
         scores = [kept([P, S], F32, f"scores{m}") for m in range(M_TILES)]
 
         def make_scores(q):
@@ -212,7 +218,7 @@ def tile_list_chip_defect_scores_kernel(
                 for s in range(2):
                     dst = scores[2 * pair + s][:, q * E_COLS : (q + 1) * E_COLS]
                     src = bank[:, s * E_COLS : (s + 1) * E_COLS]
-                    if pair == 0:
+                    if q == e_chunks - 1 and pair == 0 and s == 0:
                         nc.vector.tensor_copy(dst, src)
                     else:
                         nc.scalar.copy(dst, src)
@@ -222,40 +228,40 @@ def tile_list_chip_defect_scores_kernel(
             for c in range(J_CHUNKS):
                 x_pass(banks[c], 0, c, a)
 
-        pending = None
-        grouped1 = {}
-        for step in range(R_PASSES * J_CHUNKS):
-            b, c = divmod(step, J_CHUNKS)
-            if b == 0:
-                bank = banks[c]
-                x_pass(bank, b, c, K_PASSES - 1)
-            else:
-                bank = new_bank()
-                for a in range(K_PASSES):
-                    x_pass(bank, b, c, a)
-            h_bf = make_h(bank, b)
-            if pending is not None:
-                quantize_h(*pending)
-                pb, pc = pending[0], pending[1]
-                if pb == 1 and pc % 2 == 1:
-                    make_scores(pc // 2)
-            pending = (b, c, h_bf)
-            if step == 1:
-                grouped1[0] = round_wb(1, 0, "vector")
+        runs = [(0, 0, 1), (0, 1, 1), (0, 2, 2), (0, 4, 2), (0, 6, 2), (1, 0, 2), (1, 2, 2), (1, 4, 2), (1, 6, 1), (1, 7, 1)]
+        magnitudes, h_tiles, grouped1 = {}, {}, {}
+        for step in range(len(runs) + 2):
+            if step < len(runs):
+                b, first, count = runs[step]
+                magnitudes[step] = ring.tile([P, E_COLS, PACK], F32, name="magnitude", bufs=2)
+                for c in range(first, first + count):
+                    if b == 0:
+                        bank = banks[c]
+                        x_pass(bank, b, c, K_PASSES - 1)
+                    else:
+                        bank = new_bank()
+                        for a in range(K_PASSES):
+                            x_pass(bank, b, c, a)
+                    take_abs(bank, magnitudes[step][:, (c - first) * J : (c - first + 1) * J, :])
+            if 1 <= step <= len(runs):
+                b, first, count = runs[step - 1]
+                h_tiles[step - 1] = apply_gain(take_root(magnitudes[step - 1], count * J), b, count * J)
+            if step >= 2:
+                b, first, count = runs[step - 2]
+                quantize_h(b, first, count * J, h_tiles[step - 2])
             if step == 2:
-                quantize_wb(1, 0, grouped1[0])
+                grouped1[0] = round_wb(1, 0, "vector")
             if step == 3:
+                quantize_wb(1, 0, grouped1[0])
                 grouped1[1] = round_wb(1, 1, "vector")
             if step == 4:
                 quantize_wb(1, 1, grouped1[1])
             if step == 6:
-                nc.vector.tensor_copy(v2_scales[:], v2_scale_tab[:].indirect(idx2[:]))
-            if step == 7:
                 nc.vector.tensor_copy(v2_codes[0][:], v2_tab[0][:].bitcast(U32).indirect(idx2[:]))
-            if step == 8:
+            if step == 7:
                 nc.vector.tensor_copy(v2_codes[1][:], v2_tab[1][:].bitcast(U32).indirect(idx2[:]))
-        quantize_h(*pending)
-        make_scores(e_chunks - 1)
+            if step in (8, 9, 10, 11):
+                make_scores(step - 8)
 
         entry = [kept([P, PAIRS], F32, f"entry{m}") for m in range(M_TILES)]
         sines = {}
@@ -274,12 +280,14 @@ def tile_list_chip_defect_scores_kernel(
             sines[m] = ring.tile([P, PAIRS], F32, name="sine")
             nc.scalar.activation(sines[m][:], angle[:], ACT.Sin)
 
-        def finish(m):
+        def finish(m, first, width):
+            cols = slice(first, first + width)
             product = ring.tile([P, PAIRS], F32, name="product", bufs=2)
-            nc.vector.tensor_tensor(product[:], scores[m][:].indirect(p2[:]), sines[m][:], ALU.mult)
-            result = ring.tile([P, PAIRS], F32, name="result", bufs=2)
-            nc.scalar.activation(result[:], product[:], ACT.Identity, bias=defect_sb[:, m : m + 1], scale=-1.0)
-            nc.sync.dma_start(out=out[m * P : (m + 1) * P, :], in_=result[:])
+            window = scores[m][:].indirect(p2[:, first // 16 : (first + width) // 16])
+            nc.vector.tensor_tensor(product[:, :width], window, sines[m][:, cols], ALU.mult)
+            result = ring.tile([P, PAIRS], F32, name="result", bufs=5)
+            nc.scalar.activation(result[:, :width], product[:, :width], ACT.Identity, bias=defect_sb[:, m : m + 1], scale=-1.0)
+            nc.sync.dma_start(out=out[m * P : (m + 1) * P, cols], in_=result[:, :width])
 
         pick_entry(0)
         for m in range(M_TILES):
@@ -287,6 +295,7 @@ def tile_list_chip_defect_scores_kernel(
                 pick_entry(m + 1)
             turns = count_turns(m)
             if m > 0:
-                finish(m - 1)
+                finish(m - 1, 0, PAIRS)
             sine(m, turns)
-        finish(M_TILES - 1)
+        finish(M_TILES - 1, 0, PAIRS // 2)
+        finish(M_TILES - 1, PAIRS // 2, PAIRS // 2)

@@ -63,7 +63,7 @@ def tile_list_chip_defect_scores_kernel(
 
         v_tab = [kept([P, T], I32, f"v_tab{a}") for a in range(K_PASSES)]
         v2_tab = [kept([P, T2], I32, f"v2_tab{b}") for b in range(R_PASSES)]
-        wb_raw = [[kept([P, PACK, K_PASS], F32, f"wb_raw{b}_{a}") for a in range(2)] for b in range(R_PASSES)]
+        wb_raw = {(b, a): kept([P, PACK, K_PASS], F32, f"wb_raw{b}_{a}") for b, a in ((0, 0), (1, 0), (1, 1))}
         w4_raw = kept([P, 2 * H], U8, "w4_raw")
         idx = kept([P, S // 16], U16, "idx")
         idx2 = kept([P, S2 // 16], U16, "idx2")
@@ -77,11 +77,10 @@ def tile_list_chip_defect_scores_kernel(
 
         def load_wb(b, a):
             rows = wb[a * K_PASS : (a + 1) * K_PASS, b * K_PASS : (b + 1) * K_PASS]
-            nc.sync.dma_start(out=wb_raw[b][a][:], in_=rows.rearrange("(p i) c -> p i c", i=PACK))
+            nc.sync.dma_start(out=wb_raw[b, a][:], in_=rows.rearrange("(p i) c -> p i c", i=PACK))
 
         load_scale_rows(nc.scalar, v_scale_tab, tab_scales)
         load_scale_rows(nc.scalar, w4_scale_raw, w4_scales)
-        load_scale_rows(nc.gpsimd, v2_scale_tab, tab2_scales)
         nc.sync.dma_start(idx[:], offs)
         nc.sync.dma_start(out=gain_sb[:], in_=gain.rearrange("(b p t) -> p b t", p=P, t=PACK))
         nc.sync.dma_start(idx2[:], offs2)
@@ -90,11 +89,15 @@ def tile_list_chip_defect_scores_kernel(
         load_words(v_tab[0], tab_words[0])
         nc.sync.dma_start(out=w4_raw[:].bitcast(I32), in_=w4_words[0].bitcast(I32))
         load_wb(0, 0)
-        load_wb(0, 1)
         load_words(v_tab[1], tab_words[1])
         load_words(v_tab[2], tab_words[2])
+        last_raw = [kept([P, PACK, K_PASS // 2], F32, f"last_raw{u}") for u in range(2)]
+        for u in range(2):
+            rows = wb[K_PASS : 2 * K_PASS, u * K_PASS // 2 : (u + 1) * K_PASS // 2]
+            nc.sync.dma_start(out=last_raw[u][:], in_=rows.rearrange("(p i) c -> p i c", i=PACK))
         load_wb(1, 0)
         load_wb(1, 1)
+        load_scale_rows(nc.sync, v2_scale_tab, tab2_scales)
         load_words(v2_tab[0], tab2_words[0])
         load_words(v2_tab[1], tab2_words[1])
         with nc.allow_non_contiguous_dma(reason="one value a partition"):
@@ -117,7 +120,7 @@ def tile_list_chip_defect_scores_kernel(
         def round_wb(b, a, engine):
             grouped = ring.tile([P, PACK * K_PASS], BF16, name="wb_grouped", align_bytes=64, bufs=2)
             dst = grouped[:].rearrange("p (t m i) -> p m t i", t=PACK, i=PACK)
-            src = wb_raw[b][a][:].rearrange("p i (m t) -> p m t i", t=PACK)
+            src = wb_raw[b, a][:].rearrange("p i (m t) -> p m t i", t=PACK)
             if engine == "scalar":
                 nc.scalar.copy(dst, src)
             else:
@@ -139,13 +142,21 @@ def tile_list_chip_defect_scores_kernel(
             w4_scale_raw[:].rearrange("p (b m t) -> p b t m", b=R_PASSES, t=PACK),
         )
         g0 = round_wb(0, 0, "scalar")
-        g1 = round_wb(0, 1, "scalar")
         quantize_wb(0, 0, g0)
         gather_v(1)
-        quantize_wb(0, 1, g1)
-        v2_scales = kept([P, S2], U8, "v2_scales")
-        nc.vector.tensor_copy(v2_scales[:], v2_scale_tab[:].indirect(idx2[:]))
         gather_v(2)
+        M_HALF = P // 2
+        for u in range(2):
+            half = kept([P, PACK, M_HALF * PACK], BF16, f"last_grouped{u}")
+            dst = half[:].rearrange("p t (m i) -> p m t i", i=PACK)
+            src = last_raw[u][:].rearrange("p i (m t) -> p m t i", t=PACK)
+            if u == 0:
+                nc.scalar.copy(dst, src)
+            else:
+                nc.vector.tensor_copy(dst, src)
+            for t in range(PACK):
+                cols = slice(t * P + u * M_HALF, t * P + (u + 1) * M_HALF)
+                nc.vector.quantize_mx(out=wq_codes[0][1][:, cols].bitcast(FP8X4), scales=wq_plane[0][1][:, cols], in_=half[:, t, :])
 
         def x_pass(bank, b, c, a):
             u, col = divmod(c * J, HALF)
@@ -198,6 +209,7 @@ def tile_list_chip_defect_scores_kernel(
             )
 
         v2_codes = [kept([P, S2], U32, f"v2_codes{b}") for b in range(R_PASSES)]
+        v2_scales = kept([P, S2], U8, "v2_scales")
         scores = [kept([P, S], F32, f"scores{m}") for m in range(M_TILES)]
 
         def make_scores(q):
@@ -256,6 +268,8 @@ def tile_list_chip_defect_scores_kernel(
                 grouped1[1] = round_wb(1, 1, "vector")
             if step == 4:
                 quantize_wb(1, 1, grouped1[1])
+            if step == 5:
+                nc.vector.tensor_copy(v2_scales[:], v2_scale_tab[:].indirect(idx2[:]))
             if step == 6:
                 nc.vector.tensor_copy(v2_codes[0][:], v2_tab[0][:].bitcast(U32).indirect(idx2[:]))
             if step == 7:

@@ -19,12 +19,16 @@ PACK = 4
 K_PASS = P * PACK
 K, H, T, S, T2, S2, PAIRS = 1536, 1024, 4096, 1024, 2048, 512, 512
 K_PASSES = K // K_PASS
-R_PASSES = H // K_PASS
+WB_PASSES = K_PASSES - 1
+R_HALVES = H // K_PASS
+PER_COLUMN = 16
+PICK = 512
 J = 128
 J_CHUNKS = S // J
-E_COLS = 256
+E_COLS = 2 * J
+E_CHUNKS = S // E_COLS
 M_TILES = S2 // P
-HALF = 512
+LAST_PIECE = 128
 
 FLOPS = 2 * K * H * S + 2 * H * S2 * S
 
@@ -50,34 +54,37 @@ def tile_list_chip_defect_scores_kernel(
         def kept(shape, dtype, name):
             return keep.tile(shape, dtype, name=name, align_bytes=64)
 
+        def new_bank():
+            return psum.tile([P, PACK * J], F32, name="bank")
+
         v_scale_tab = kept([P, T], U8, "v_scale_tab")
         w4_scale_raw = kept([P, H], U8, "w4_scale_raw")
         v2_scale_tab = kept([P, T2], U8, "v2_scale_tab")
         one = kept([P, 1], F32, "one")
-        warm = kept([P, 1], F32, "warm")
         nc.vector.memset(v_scale_tab[:].bitcast(I32), 0)
         nc.vector.memset(w4_scale_raw[:].bitcast(I32), 0)
         nc.vector.memset(v2_scale_tab[:].bitcast(I32), 0)
         nc.vector.memset(one[:], 1.0)
-        nc.scalar.activation(warm[:], one[:], ACT.Sqrt, bias=one[:])
+        zero = kept([P, 1], F32, "zero")
+        nc.scalar.activation(zero[:], one[:], ACT.Sqrt, bias=one[:], scale=-1.0)
 
         v_tab = [kept([P, T], I32, f"v_tab{a}") for a in range(K_PASSES)]
-        v2_tab = [kept([P, T2], I32, f"v2_tab{b}") for b in range(R_PASSES)]
-        wb_raw = {(b, a): kept([P, PACK, K_PASS], F32, f"wb_raw{b}_{a}") for b, a in ((0, 0), (1, 0), (1, 1))}
+        v2_tab = [kept([P, T2], I32, f"v2_tab{b}") for b in range(R_HALVES)]
+        wb_raw = {(b, n): kept([P, PACK, K_PASS], F32, f"wb_raw{b}_{n}") for b, n in ((0, 0), (1, 0), (1, 1))}
         w4_raw = kept([P, 2 * H], U8, "w4_raw")
-        idx = kept([P, S // 16], U16, "idx")
-        idx2 = kept([P, S2 // 16], U16, "idx2")
-        p1 = kept([P, PAIRS // 16], U16, "p1")
-        p2 = kept([P, PAIRS // 16], U16, "p2")
-        gain_sb = kept([P, R_PASSES, PACK], F32, "gain_sb")
+        idx = kept([P, S // PER_COLUMN], U16, "idx")
+        idx2 = kept([P, S2 // PER_COLUMN], U16, "idx2")
+        p1 = kept([P, PAIRS // PER_COLUMN], U16, "p1")
+        p2 = kept([P, PAIRS // PER_COLUMN], U16, "p2")
+        gain_sb = kept([P, R_HALVES, PACK], F32, "gain_sb")
         defect_sb = kept([P, M_TILES], F32, "defect_sb")
 
         def load_words(tile, words):
             nc.sync.dma_start(out=tile[:], in_=words.rearrange("p t i -> p (t i)").bitcast(I32))
 
-        def load_wb(b, a):
-            rows = wb[a * K_PASS : (a + 1) * K_PASS, b * K_PASS : (b + 1) * K_PASS]
-            nc.sync.dma_start(out=wb_raw[b, a][:], in_=rows.rearrange("(p i) c -> p i c", i=PACK))
+        def load_wb(tile, n, first_column):
+            rows = wb[n * K_PASS : (n + 1) * K_PASS, first_column : first_column + tile.shape[2]]
+            nc.sync.dma_start(out=tile[:], in_=rows.rearrange("(p i) c -> p i c", i=PACK))
 
         load_scale_rows(nc.scalar, v_scale_tab, tab_scales)
         load_scale_rows(nc.scalar, w4_scale_raw, w4_scales)
@@ -88,106 +95,97 @@ def tile_list_chip_defect_scores_kernel(
         nc.sync.dma_start(p2[:], pos2)
         load_words(v_tab[0], tab_words[0])
         nc.sync.dma_start(out=w4_raw[:].bitcast(I32), in_=w4_words[0].bitcast(I32))
-        load_wb(0, 0)
+        load_wb(wb_raw[0, 0], 0, 0)
         load_words(v_tab[1], tab_words[1])
         load_words(v_tab[2], tab_words[2])
         last_raw = [kept([P, PACK, K_PASS // 2], F32, f"last_raw{u}") for u in range(2)]
         for u in range(2):
-            rows = wb[K_PASS : 2 * K_PASS, u * K_PASS // 2 : (u + 1) * K_PASS // 2]
-            nc.sync.dma_start(out=last_raw[u][:], in_=rows.rearrange("(p i) c -> p i c", i=PACK))
-        load_wb(1, 0)
-        load_wb(1, 1)
+            load_wb(last_raw[u], 1, u * K_PASS // 2)
+        load_wb(wb_raw[1, 0], 0, K_PASS)
+        load_wb(wb_raw[1, 1], 1, K_PASS)
         load_scale_rows(nc.sync, v2_scale_tab, tab2_scales)
         load_words(v2_tab[0], tab2_words[0])
         load_words(v2_tab[1], tab2_words[1])
-        with nc.allow_non_contiguous_dma(reason="one value a partition"):
+        with nc.allow_non_contiguous_dma(reason="one value a partition for each tile of m"):
             nc.sync.dma_start(out=defect_sb[:], in_=defect.rearrange("(t p) -> p t", p=P))
 
-
-        v_codes = [[kept([P, HALF], U32, f"v_codes{a}_{u}") for u in range(2)] for a in range(K_PASSES)]
+        v_codes = [[kept([P, PICK], U32, f"v_codes{a}_{u}") for u in range(S // PICK)] for a in range(K_PASSES)]
         v_scales = kept([P, S], U8, "v_scales")
+        w4_codes = kept([P, 2 * H], U8, "w4_codes")
+        w4_scale = kept([P, H], U8, "w4_scale")
+        wq_codes = [[kept([P, K_PASS], U32, f"wq_codes{b}_{n}") for n in range(WB_PASSES)] for b in range(R_HALVES)]
+        wq_scale = [[kept([P, K_PASS], U8, f"wq_scale{b}_{n}") for n in range(WB_PASSES)] for b in range(R_HALVES)]
+        wb_rounded = {}
 
         def gather_v(a):
-            for u in range(2):
-                cols = idx[:, u * HALF // 16 : (u + 1) * HALF // 16]
-                nc.vector.tensor_copy(v_codes[a][u][:], v_tab[a][:].bitcast(U32).indirect(cols))
+            for u in range(S // PICK):
+                entries = idx[:, u * PICK // PER_COLUMN : (u + 1) * PICK // PER_COLUMN]
+                nc.vector.tensor_copy(v_codes[a][u][:], v_tab[a][:].bitcast(U32).indirect(entries))
 
-        w4_codes = kept([P, 2 * H], U8, "w4_codes")
-        w4_plane = kept([P, H], U8, "w4_plane")
-        wq_codes = [[kept([P, K_PASS], U32, f"wq_codes{b}_{a}") for a in range(2)] for b in range(R_PASSES)]
-        wq_plane = [[kept([P, K_PASS], U8, f"wq_plane{b}_{a}") for a in range(2)] for b in range(R_PASSES)]
+        def round_wb(b, n, copy):
+            rounded = ring.tile([P, PACK * K_PASS], BF16, name="wb_rounded", align_bytes=64, bufs=2)
+            copy(
+                rounded[:].rearrange("p (t c i) -> p c t i", t=PACK, i=PACK),
+                wb_raw[b, n][:].rearrange("p i (c t) -> p c t i", t=PACK),
+            )
+            wb_rounded[b, n] = rounded
 
-        def round_wb(b, a, engine):
-            grouped = ring.tile([P, PACK * K_PASS], BF16, name="wb_grouped", align_bytes=64, bufs=2)
-            dst = grouped[:].rearrange("p (t m i) -> p m t i", t=PACK, i=PACK)
-            src = wb_raw[b, a][:].rearrange("p i (m t) -> p m t i", t=PACK)
-            if engine == "scalar":
-                nc.scalar.copy(dst, src)
-            else:
-                nc.vector.tensor_copy(dst, src)
-            return grouped
-
-        def quantize_wb(b, a, grouped):
-            nc.vector.quantize_mx(out=wq_codes[b][a][:].bitcast(FP8X4), scales=wq_plane[b][a][:], in_=grouped[:])
+        def quantize_wb(b, n):
+            nc.vector.quantize_mx(out=wq_codes[b][n][:].bitcast(FP8X4), scales=wq_scale[b][n][:], in_=wb_rounded[b, n][:])
 
         gather_v(0)
         nc.vector.tensor_copy(v_scales[:], v_scale_tab[:].indirect(idx[:]))
-        for b in range(R_PASSES):
+        for b in range(R_HALVES):
             nc.vector.tensor_copy(
-                w4_codes[:, b * 2 * K_PASS : (b + 1) * 2 * K_PASS].rearrange("p (t m e) -> p t m e", t=PACK, e=2),
-                w4_raw[:, b * 2 * K_PASS : (b + 1) * 2 * K_PASS].rearrange("p (m t e) -> p t m e", t=PACK, e=2),
+                w4_codes[:, b * 2 * K_PASS : (b + 1) * 2 * K_PASS].rearrange("p (t c e) -> p t c e", t=PACK, e=2),
+                w4_raw[:, b * 2 * K_PASS : (b + 1) * 2 * K_PASS].rearrange("p (c t e) -> p t c e", t=PACK, e=2),
             )
         nc.vector.tensor_copy(
-            w4_plane[:].rearrange("p (b t m) -> p b t m", b=R_PASSES, t=PACK),
-            w4_scale_raw[:].rearrange("p (b m t) -> p b t m", b=R_PASSES, t=PACK),
+            w4_scale[:].rearrange("p (b t c) -> p b t c", b=R_HALVES, t=PACK),
+            w4_scale_raw[:].rearrange("p (b c t) -> p b t c", b=R_HALVES, t=PACK),
         )
-        g0 = round_wb(0, 0, "scalar")
-        quantize_wb(0, 0, g0)
+        round_wb(0, 0, nc.scalar.copy)
+        quantize_wb(0, 0)
         gather_v(1)
         gather_v(2)
-        M_HALF = P // 2
-        for u in range(2):
-            half = kept([P, PACK, M_HALF * PACK], BF16, f"last_grouped{u}")
-            dst = half[:].rearrange("p t (m i) -> p m t i", i=PACK)
-            src = last_raw[u][:].rearrange("p i (m t) -> p m t i", t=PACK)
-            if u == 0:
-                nc.scalar.copy(dst, src)
-            else:
-                nc.vector.tensor_copy(dst, src)
+        places = P // 2
+        for u, copy in enumerate((nc.scalar.copy, nc.vector.tensor_copy)):
+            last_rounded = kept([P, PACK, places * PACK], BF16, f"last_rounded{u}")
+            copy(
+                last_rounded[:].rearrange("p t (c i) -> p c t i", i=PACK),
+                last_raw[u][:].rearrange("p i (c t) -> p c t i", t=PACK),
+            )
             for t in range(PACK):
-                cols = slice(t * P + u * M_HALF, t * P + (u + 1) * M_HALF)
-                nc.vector.quantize_mx(out=wq_codes[0][1][:, cols].bitcast(FP8X4), scales=wq_plane[0][1][:, cols], in_=half[:, t, :])
+                cols = slice(t * P + u * places, t * P + (u + 1) * places)
+                nc.vector.quantize_mx(
+                    out=wq_codes[0][1][:, cols].bitcast(FP8X4), scales=wq_scale[0][1][:, cols], in_=last_rounded[:, t, :]
+                )
 
-        def x_pass(bank, b, c, a):
-            u, col = divmod(c * J, HALF)
+        def x_pass(bank, b, chunk, a):
+            u, col = divmod(chunk * J, PICK)
             for t in range(PACK):
-                m0 = t * P
                 if a == 0:
-                    w0 = b * K_PASS + m0
+                    w0 = b * K_PASS + t * P
                     lhs = w4_codes[:, 2 * w0 : 2 * (w0 + P)].bitcast(FP4X4)
-                    lhs_scale = w4_plane[:, w0 : w0 + P]
+                    lhs_scale = w4_scale[:, w0 : w0 + P]
                 else:
-                    lhs = wq_codes[b][a - 1][:, m0 : m0 + P].bitcast(FP8X4)
-                    lhs_scale = wq_plane[b][a - 1][:, m0 : m0 + P]
+                    lhs = wq_codes[b][a - 1][:, t * P : (t + 1) * P].bitcast(FP8X4)
+                    lhs_scale = wq_scale[b][a - 1][:, t * P : (t + 1) * P]
                 nc.tensor.matmul_mx(
                     out=bank[:, t * J : (t + 1) * J],
                     lhsT=lhs,
                     lhsT_scale=lhs_scale,
                     rhs=v_codes[a][u][:, col : col + J].bitcast(FP8X4),
-                    rhs_scale=v_scales[4 * a :, c * J : (c + 1) * J],
+                    rhs_scale=v_scales[4 * a :, chunk * J : (chunk + 1) * J],
                     start=(a == 0 and t == 0),
                     stop=(a == K_PASSES - 1 and t == PACK - 1),
                 )
 
-        def new_bank():
-            return psum.tile([P, PACK * J], F32, name="bank")
-
-        e_chunks = S // E_COLS
-        h_codes = [[kept([P, E_COLS], U32, f"h_codes{b}_{q}") for q in range(e_chunks)] for b in range(R_PASSES)]
-        h_plane = [[kept([P, E_COLS], U8, f"h_plane{b}_{q}") for q in range(e_chunks)] for b in range(R_PASSES)]
+        h_codes = [[kept([P, E_COLS], U32, f"h_codes{b}_{q}") for q in range(E_CHUNKS)] for b in range(R_HALVES)]
+        h_scale = [[kept([P, E_COLS], U8, f"h_scale{b}_{q}") for q in range(E_CHUNKS)] for b in range(R_HALVES)]
 
         def take_abs(bank, magnitude):
-            nc.scalar.activation(magnitude, bank[:].rearrange("p (t j) -> p j t", t=PACK), ACT.Abs)
+            nc.scalar.activation(magnitude, bank[:].rearrange("p (t j) -> p j t", t=PACK), ACT.Abs, bias=zero[:])
 
         def take_root(magnitude, width):
             root = ring.tile([P, E_COLS, PACK], F32, name="root")
@@ -195,121 +193,131 @@ def tile_list_chip_defect_scores_kernel(
             return root
 
         def apply_gain(root, b, width):
-            h_bf = ring.tile([P, E_COLS, PACK], BF16, name="h_bf", align_bytes=64, bufs=2)
+            h_rounded = ring.tile([P, E_COLS, PACK], BF16, name="h_rounded", align_bytes=64, bufs=2)
             gains = gain_sb[:, b : b + 1, :].broadcast_to([P, width, PACK])
-            nc.vector.tensor_tensor(h_bf[:, :width, :], root[:, :width, :], gains, ALU.mult)
-            return h_bf
+            nc.vector.tensor_tensor(h_rounded[:, :width, :], root[:, :width, :], gains, ALU.mult)
+            return h_rounded
 
-        def quantize_h(b, c, width, h_bf):
-            q, col = divmod(c * J, E_COLS)
+        def quantize_h(b, chunk, width, h_rounded):
+            q, col = divmod(chunk * J, E_COLS)
             nc.vector.quantize_mx(
                 out=h_codes[b][q][:, col : col + width].bitcast(FP8X4),
-                scales=h_plane[b][q][:, col : col + width],
-                in_=h_bf[:, :width, :].rearrange("p j t -> p (j t)"),
+                scales=h_scale[b][q][:, col : col + width],
+                in_=h_rounded[:, :width, :].rearrange("p j t -> p (j t)"),
             )
 
-        v2_codes = [kept([P, S2], U32, f"v2_codes{b}") for b in range(R_PASSES)]
+        v2_codes = [kept([P, S2], U32, f"v2_codes{b}") for b in range(R_HALVES)]
         v2_scales = kept([P, S2], U8, "v2_scales")
         scores = [kept([P, S], F32, f"scores{m}") for m in range(M_TILES)]
+        score_banks = {}
+
+        def gather_v2_scales():
+            nc.vector.tensor_copy(v2_scales[:], v2_scale_tab[:].indirect(idx2[:]))
+
+        def gather_v2(b):
+            nc.vector.tensor_copy(v2_codes[b][:], v2_tab[b][:].bitcast(U32).indirect(idx2[:]))
+
+        def score_pass(q, pair, b, first, width, start, stop):
+            for side in range(2):
+                m0 = (2 * pair + side) * P
+                nc.tensor.matmul_mx(
+                    out=score_banks[q, pair][:, side * E_COLS + first : side * E_COLS + first + width],
+                    lhsT=v2_codes[b][:, m0 : m0 + P].bitcast(FP8X4),
+                    lhsT_scale=v2_scales[4 * b :, m0 : m0 + P],
+                    rhs=h_codes[b][q][:, first : first + width].bitcast(FP8X4),
+                    rhs_scale=h_scale[b][q][:, first : first + width],
+                    start=(start and side == 0),
+                    stop=(stop and side == 1),
+                )
 
         def make_scores(q):
+            is_last = q == E_CHUNKS - 1
             for pair in range(M_TILES // 2):
-                bank = new_bank()
-                for b in range(R_PASSES):
-                    for s in range(2):
-                        m0 = (2 * pair + s) * P
-                        nc.tensor.matmul_mx(
-                            out=bank[:, s * E_COLS : (s + 1) * E_COLS],
-                            lhsT=v2_codes[b][:, m0 : m0 + P].bitcast(FP8X4),
-                            lhsT_scale=v2_scales[4 * b :, m0 : m0 + P],
-                            rhs=h_codes[b][q][:].bitcast(FP8X4),
-                            rhs_scale=h_plane[b][q][:],
-                            start=(b == 0 and s == 0),
-                            stop=(b == R_PASSES - 1 and s == 1),
-                        )
-                for s in range(2):
-                    dst = scores[2 * pair + s][:, q * E_COLS : (q + 1) * E_COLS]
-                    src = bank[:, s * E_COLS : (s + 1) * E_COLS]
-                    if q == e_chunks - 1 and pair == 0 and s == 0:
-                        nc.vector.tensor_copy(dst, src)
-                    else:
-                        nc.scalar.copy(dst, src)
+                score_banks[q, pair] = new_bank()
+                score_pass(q, pair, 0, 0, E_COLS, True, False)
+                score_pass(q, pair, 1, 0, J if is_last else E_COLS, False, not is_last)
+            if is_last:
+                for pair in range(M_TILES // 2):
+                    score_pass(q, pair, 1, J, J, False, True)
 
-        banks = [new_bank() for c in range(J_CHUNKS)]
+        first_banks = [new_bank() for chunk in range(J_CHUNKS)]
         for a in range(K_PASSES - 1):
-            for c in range(J_CHUNKS):
-                x_pass(banks[c], 0, c, a)
+            for chunk in range(J_CHUNKS):
+                x_pass(first_banks[chunk], 0, chunk, a)
 
-        runs = [(0, 0, 1), (0, 1, 1), (0, 2, 2), (0, 4, 2), (0, 6, 2), (1, 0, 2), (1, 2, 2), (1, 4, 2), (1, 6, 1), (1, 7, 1)]
-        magnitudes, h_tiles, grouped1 = {}, {}, {}
+        runs = [(b, chunk, 2) for b in range(R_HALVES) for chunk in range(0, J_CHUNKS, 2)]
+        runs = [(0, 0, 1), (0, 1, 1)] + runs[1:-1] + [(R_HALVES - 1, J_CHUNKS - 2, 1), (R_HALVES - 1, J_CHUNKS - 1, 1)]
+        side_work = [
+            lambda: round_wb(1, 0, nc.vector.tensor_copy),
+            lambda: (quantize_wb(1, 0), round_wb(1, 1, nc.vector.tensor_copy)),
+            lambda: quantize_wb(1, 1),
+            gather_v2_scales,
+            lambda: gather_v2(0),
+            lambda: gather_v2(1),
+        ] + [lambda q=q: make_scores(q) for q in range(E_CHUNKS)]
+
+        magnitudes, h_tiles = {}, {}
         for step in range(len(runs) + 2):
             if step < len(runs):
                 b, first, count = runs[step]
                 magnitudes[step] = ring.tile([P, E_COLS, PACK], F32, name="magnitude", bufs=2)
-                for c in range(first, first + count):
+                for chunk in range(first, first + count):
                     if b == 0:
-                        bank = banks[c]
-                        x_pass(bank, b, c, K_PASSES - 1)
+                        bank = first_banks[chunk]
+                        x_pass(bank, b, chunk, K_PASSES - 1)
                     else:
                         bank = new_bank()
                         for a in range(K_PASSES):
-                            x_pass(bank, b, c, a)
-                    take_abs(bank, magnitudes[step][:, (c - first) * J : (c - first + 1) * J, :])
+                            x_pass(bank, b, chunk, a)
+                    take_abs(bank, magnitudes[step][:, (chunk - first) * J : (chunk - first + 1) * J, :])
             if 1 <= step <= len(runs):
                 b, first, count = runs[step - 1]
                 h_tiles[step - 1] = apply_gain(take_root(magnitudes[step - 1], count * J), b, count * J)
             if step >= 2:
                 b, first, count = runs[step - 2]
                 quantize_h(b, first, count * J, h_tiles[step - 2])
-            if step == 2:
-                grouped1[0] = round_wb(1, 0, "vector")
-            if step == 3:
-                quantize_wb(1, 0, grouped1[0])
-                grouped1[1] = round_wb(1, 1, "vector")
-            if step == 4:
-                quantize_wb(1, 1, grouped1[1])
-            if step == 5:
-                nc.vector.tensor_copy(v2_scales[:], v2_scale_tab[:].indirect(idx2[:]))
-            if step == 6:
-                nc.vector.tensor_copy(v2_codes[0][:], v2_tab[0][:].bitcast(U32).indirect(idx2[:]))
-            if step == 7:
-                nc.vector.tensor_copy(v2_codes[1][:], v2_tab[1][:].bitcast(U32).indirect(idx2[:]))
-            if step in (8, 9, 10, 11):
-                make_scores(step - 8)
+                side_work[step - 2]()
+
+        for m in range(M_TILES):
+            pair, side = divmod(m, 2)
+            for q in range(E_CHUNKS):
+                copy = nc.vector.tensor_copy if (m == 0 and q == E_CHUNKS - 1) else nc.scalar.copy
+                copy(scores[m][:, q * E_COLS : (q + 1) * E_COLS], score_banks[q, pair][:, side * E_COLS : (side + 1) * E_COLS])
 
         entry = [kept([P, PAIRS], F32, f"entry{m}") for m in range(M_TILES)]
-        sines = {}
+        turns, sines = {}, {}
 
         def pick_entry(m):
             nc.vector.tensor_copy(entry[m][:], scores[m][:].indirect(p1[:]))
 
         def count_turns(m):
-            turns = ring.tile([P, PAIRS], I32, name="turns", bufs=2)
-            nc.vector.tensor_scalar(turns[:], entry[m][:], 1.0 / (2.0 * math.pi), None, ALU.mult)
-            return turns
+            turns[m] = ring.tile([P, PAIRS], I32, name="turns", bufs=2)
+            nc.vector.tensor_scalar(turns[m][:], entry[m][:], 1.0 / (2.0 * math.pi), None, ALU.mult)
 
-        def sine(m, turns):
+        def take_sine(m):
             angle = ring.tile([P, PAIRS], F32, name="angle", bufs=2)
-            nc.vector.scalar_tensor_tensor(angle[:], turns[:], -2.0 * math.pi, entry[m][:], ALU.mult, ALU.add)
+            nc.vector.scalar_tensor_tensor(angle[:], turns[m][:], -2.0 * math.pi, entry[m][:], ALU.mult, ALU.add)
             sines[m] = ring.tile([P, PAIRS], F32, name="sine")
             nc.scalar.activation(sines[m][:], angle[:], ACT.Sin)
 
         def finish(m, first, width):
             cols = slice(first, first + width)
             product = ring.tile([P, PAIRS], F32, name="product", bufs=2)
-            window = scores[m][:].indirect(p2[:, first // 16 : (first + width) // 16])
-            nc.vector.tensor_tensor(product[:, :width], window, sines[m][:, cols], ALU.mult)
-            result = ring.tile([P, PAIRS], F32, name="result", bufs=5)
+            exits = scores[m][:].indirect(p2[:, first // PER_COLUMN : (first + width) // PER_COLUMN])
+            nc.vector.tensor_tensor(product[:, :width], exits, sines[m][:, cols], ALU.mult)
+            result = ring.tile([P, PAIRS], F32, name="result", bufs=M_TILES + 1)
             nc.scalar.activation(result[:, :width], product[:, :width], ACT.Identity, bias=defect_sb[:, m : m + 1], scale=-1.0)
             nc.sync.dma_start(out=out[m * P : (m + 1) * P, cols], in_=result[:, :width])
 
         pick_entry(0)
+        pick_entry(1)
         for m in range(M_TILES):
-            if m + 1 < M_TILES:
-                pick_entry(m + 1)
-            turns = count_turns(m)
-            if m > 0:
-                finish(m - 1, 0, PAIRS)
-            sine(m, turns)
-        finish(M_TILES - 1, 0, PAIRS // 2)
-        finish(M_TILES - 1, PAIRS // 2, PAIRS // 2)
+            count_turns(m)
+            if m + 2 < M_TILES:
+                pick_entry(m + 2)
+            else:
+                finish(m - 2, 0, PAIRS)
+            take_sine(m)
+        finish(M_TILES - 2, 0, PAIRS)
+        finish(M_TILES - 1, 0, PAIRS - LAST_PIECE)
+        finish(M_TILES - 1, PAIRS - LAST_PIECE, LAST_PIECE)

import math
from contextlib import ExitStack

import concourse.mybir as mybir

F32 = mybir.dt.float32
BF16 = mybir.dt.bfloat16
I32 = mybir.dt.int32
U32 = mybir.dt.uint32
U16 = mybir.dt.uint16
U8 = mybir.dt.uint8
FP8X4 = mybir.dt.float8_e4m3fn_x4
FP4X4 = mybir.dt.float4_e2m1fn_x4
ACT = mybir.ActivationFunctionType
ALU = mybir.AluOpType

P = 128
PACK = 4
K_PASS = P * PACK
K, H, T, S, T2, S2, PAIRS = 1536, 1024, 4096, 1024, 2048, 512, 512
K_PASSES = K // K_PASS
WB_PASSES = K_PASSES - 1
R_HALVES = H // K_PASS
PER_COLUMN = 16
PICK = 512
J = 128
J_CHUNKS = S // J
E_COLS = 2 * J
E_CHUNKS = S // E_COLS
M_TILES = S2 // P
LAST_PIECE = 128

FLOPS = 2 * K * H * S + 2 * H * S2 * S


def load_scale_rows(queue, plane, scales):
    passes = scales.shape[0]
    for quadrant in range(4):
        queue.dma_start(
            out=plane[32 * quadrant : 32 * quadrant + 4 * passes, :].bitcast(I32),
            in_=scales[:, 4 * quadrant : 4 * quadrant + 4, :].bitcast(I32),
        )


def tile_list_chip_defect_scores_kernel(
    tc, tab_words, tab_scales, offs, tab2_words, tab2_scales, offs2, pos1, pos2, w4_words, w4_scales, wb, gain, defect, out
):
    nc = tc.nc
    with ExitStack() as ctx:
        keep = ctx.enter_context(tc.tile_pool(name="keep", bufs=1))
        ring = ctx.enter_context(tc.tile_pool(name="ring", bufs=3))
        psum = ctx.enter_context(tc.psum_pool(name="psum", bufs=8))

        def kept(shape, dtype, name):
            return keep.tile(shape, dtype, name=name, align_bytes=64)

        def new_bank():
            return psum.tile([P, PACK * J], F32, name="bank")

        v_scale_tab = kept([P, T], U8, "v_scale_tab")
        w4_scale_raw = kept([P, H], U8, "w4_scale_raw")
        v2_scale_tab = kept([P, T2], U8, "v2_scale_tab")
        one = kept([P, 1], F32, "one")
        nc.vector.memset(v_scale_tab[:].bitcast(I32), 0)
        nc.vector.memset(w4_scale_raw[:].bitcast(I32), 0)
        nc.vector.memset(v2_scale_tab[:].bitcast(I32), 0)
        nc.vector.memset(one[:], 1.0)
        zero = kept([P, 1], F32, "zero")
        nc.scalar.activation(zero[:], one[:], ACT.Sqrt, bias=one[:], scale=-1.0)

        v_tab = [kept([P, T], I32, f"v_tab{a}") for a in range(K_PASSES)]
        v2_tab = [kept([P, T2], I32, f"v2_tab{b}") for b in range(R_HALVES)]
        wb_raw = {(b, n): kept([P, PACK, K_PASS], F32, f"wb_raw{b}_{n}") for b, n in ((0, 0), (1, 0), (1, 1))}
        w4_raw = kept([P, 2 * H], U8, "w4_raw")
        idx = kept([P, S // PER_COLUMN], U16, "idx")
        idx2 = kept([P, S2 // PER_COLUMN], U16, "idx2")
        p1 = kept([P, PAIRS // PER_COLUMN], U16, "p1")
        p2 = kept([P, PAIRS // PER_COLUMN], U16, "p2")
        gain_sb = kept([P, R_HALVES, PACK], F32, "gain_sb")
        defect_sb = kept([P, M_TILES], F32, "defect_sb")

        def load_words(tile, words):
            nc.sync.dma_start(out=tile[:], in_=words.rearrange("p t i -> p (t i)").bitcast(I32))

        def load_wb(tile, n, first_column):
            rows = wb[n * K_PASS : (n + 1) * K_PASS, first_column : first_column + tile.shape[2]]
            nc.sync.dma_start(out=tile[:], in_=rows.rearrange("(p i) c -> p i c", i=PACK))

        load_scale_rows(nc.scalar, v_scale_tab, tab_scales)
        load_scale_rows(nc.scalar, w4_scale_raw, w4_scales)
        nc.sync.dma_start(idx[:], offs)
        nc.sync.dma_start(out=gain_sb[:], in_=gain.rearrange("(b p t) -> p b t", p=P, t=PACK))
        nc.sync.dma_start(idx2[:], offs2)
        nc.sync.dma_start(p1[:], pos1)
        nc.sync.dma_start(p2[:], pos2)
        load_words(v_tab[0], tab_words[0])
        nc.sync.dma_start(out=w4_raw[:].bitcast(I32), in_=w4_words[0].bitcast(I32))
        load_wb(wb_raw[0, 0], 0, 0)
        load_words(v_tab[1], tab_words[1])
        load_words(v_tab[2], tab_words[2])
        last_raw = [kept([P, PACK, K_PASS // 2], F32, f"last_raw{u}") for u in range(2)]
        for u in range(2):
            load_wb(last_raw[u], 1, u * K_PASS // 2)
        load_wb(wb_raw[1, 0], 0, K_PASS)
        load_wb(wb_raw[1, 1], 1, K_PASS)
        load_scale_rows(nc.sync, v2_scale_tab, tab2_scales)
        load_words(v2_tab[0], tab2_words[0])
        load_words(v2_tab[1], tab2_words[1])
        with nc.allow_non_contiguous_dma(reason="one value a partition for each tile of m"):
            nc.sync.dma_start(out=defect_sb[:], in_=defect.rearrange("(t p) -> p t", p=P))

        v_codes = [[kept([P, PICK], U32, f"v_codes{a}_{u}") for u in range(S // PICK)] for a in range(K_PASSES)]
        v_scales = kept([P, S], U8, "v_scales")
        w4_codes = kept([P, 2 * H], U8, "w4_codes")
        w4_scale = kept([P, H], U8, "w4_scale")
        wq_codes = [[kept([P, K_PASS], U32, f"wq_codes{b}_{n}") for n in range(WB_PASSES)] for b in range(R_HALVES)]
        wq_scale = [[kept([P, K_PASS], U8, f"wq_scale{b}_{n}") for n in range(WB_PASSES)] for b in range(R_HALVES)]
        wb_rounded = {}

        def gather_v(a):
            for u in range(S // PICK):
                entries = idx[:, u * PICK // PER_COLUMN : (u + 1) * PICK // PER_COLUMN]
                nc.vector.tensor_copy(v_codes[a][u][:], v_tab[a][:].bitcast(U32).indirect(entries))

        def round_wb(b, n, copy):
            rounded = ring.tile([P, PACK * K_PASS], BF16, name="wb_rounded", align_bytes=64, bufs=2)
            copy(
                rounded[:].rearrange("p (t c i) -> p c t i", t=PACK, i=PACK),
                wb_raw[b, n][:].rearrange("p i (c t) -> p c t i", t=PACK),
            )
            wb_rounded[b, n] = rounded

        def quantize_wb(b, n):
            nc.vector.quantize_mx(out=wq_codes[b][n][:].bitcast(FP8X4), scales=wq_scale[b][n][:], in_=wb_rounded[b, n][:])

        gather_v(0)
        nc.vector.tensor_copy(v_scales[:], v_scale_tab[:].indirect(idx[:]))
        for b in range(R_HALVES):
            nc.vector.tensor_copy(
                w4_codes[:, b * 2 * K_PASS : (b + 1) * 2 * K_PASS].rearrange("p (t c e) -> p t c e", t=PACK, e=2),
                w4_raw[:, b * 2 * K_PASS : (b + 1) * 2 * K_PASS].rearrange("p (c t e) -> p t c e", t=PACK, e=2),
            )
        nc.vector.tensor_copy(
            w4_scale[:].rearrange("p (b t c) -> p b t c", b=R_HALVES, t=PACK),
            w4_scale_raw[:].rearrange("p (b c t) -> p b t c", b=R_HALVES, t=PACK),
        )
        round_wb(0, 0, nc.scalar.copy)
        quantize_wb(0, 0)
        gather_v(1)
        gather_v(2)
        places = P // 2
        for u, copy in enumerate((nc.scalar.copy, nc.vector.tensor_copy)):
            last_rounded = kept([P, PACK, places * PACK], BF16, f"last_rounded{u}")
            copy(
                last_rounded[:].rearrange("p t (c i) -> p c t i", i=PACK),
                last_raw[u][:].rearrange("p i (c t) -> p c t i", t=PACK),
            )
            for t in range(PACK):
                cols = slice(t * P + u * places, t * P + (u + 1) * places)
                nc.vector.quantize_mx(
                    out=wq_codes[0][1][:, cols].bitcast(FP8X4), scales=wq_scale[0][1][:, cols], in_=last_rounded[:, t, :]
                )

        def x_pass(bank, b, chunk, a):
            u, col = divmod(chunk * J, PICK)
            for t in range(PACK):
                if a == 0:
                    w0 = b * K_PASS + t * P
                    lhs = w4_codes[:, 2 * w0 : 2 * (w0 + P)].bitcast(FP4X4)
                    lhs_scale = w4_scale[:, w0 : w0 + P]
                else:
                    lhs = wq_codes[b][a - 1][:, t * P : (t + 1) * P].bitcast(FP8X4)
                    lhs_scale = wq_scale[b][a - 1][:, t * P : (t + 1) * P]
                nc.tensor.matmul_mx(
                    out=bank[:, t * J : (t + 1) * J],
                    lhsT=lhs,
                    lhsT_scale=lhs_scale,
                    rhs=v_codes[a][u][:, col : col + J].bitcast(FP8X4),
                    rhs_scale=v_scales[4 * a :, chunk * J : (chunk + 1) * J],
                    start=(a == 0 and t == 0),
                    stop=(a == K_PASSES - 1 and t == PACK - 1),
                )

        h_codes = [[kept([P, E_COLS], U32, f"h_codes{b}_{q}") for q in range(E_CHUNKS)] for b in range(R_HALVES)]
        h_scale = [[kept([P, E_COLS], U8, f"h_scale{b}_{q}") for q in range(E_CHUNKS)] for b in range(R_HALVES)]

        def take_abs(bank, magnitude):
            nc.scalar.activation(magnitude, bank[:].rearrange("p (t j) -> p j t", t=PACK), ACT.Abs, bias=zero[:])

        def take_root(magnitude, width):
            root = ring.tile([P, E_COLS, PACK], F32, name="root")
            nc.scalar.activation(root[:, :width, :], magnitude[:, :width, :], ACT.Sqrt, bias=one[:])
            return root

        def apply_gain(root, b, width):
            h_rounded = ring.tile([P, E_COLS, PACK], BF16, name="h_rounded", align_bytes=64, bufs=2)
            gains = gain_sb[:, b : b + 1, :].broadcast_to([P, width, PACK])
            nc.vector.tensor_tensor(h_rounded[:, :width, :], root[:, :width, :], gains, ALU.mult)
            return h_rounded

        def quantize_h(b, chunk, width, h_rounded):
            q, col = divmod(chunk * J, E_COLS)
            nc.vector.quantize_mx(
                out=h_codes[b][q][:, col : col + width].bitcast(FP8X4),
                scales=h_scale[b][q][:, col : col + width],
                in_=h_rounded[:, :width, :].rearrange("p j t -> p (j t)"),
            )

        v2_codes = [kept([P, S2], U32, f"v2_codes{b}") for b in range(R_HALVES)]
        v2_scales = kept([P, S2], U8, "v2_scales")
        scores = [kept([P, S], F32, f"scores{m}") for m in range(M_TILES)]
        score_banks = {}

        def gather_v2_scales():
            nc.vector.tensor_copy(v2_scales[:], v2_scale_tab[:].indirect(idx2[:]))

        def gather_v2(b):
            nc.vector.tensor_copy(v2_codes[b][:], v2_tab[b][:].bitcast(U32).indirect(idx2[:]))

        def score_pass(q, pair, b, first, width, start, stop):
            for side in range(2):
                m0 = (2 * pair + side) * P
                nc.tensor.matmul_mx(
                    out=score_banks[q, pair][:, side * E_COLS + first : side * E_COLS + first + width],
                    lhsT=v2_codes[b][:, m0 : m0 + P].bitcast(FP8X4),
                    lhsT_scale=v2_scales[4 * b :, m0 : m0 + P],
                    rhs=h_codes[b][q][:, first : first + width].bitcast(FP8X4),
                    rhs_scale=h_scale[b][q][:, first : first + width],
                    start=(start and side == 0),
                    stop=(stop and side == 1),
                )

        def make_scores(q):
            is_last = q == E_CHUNKS - 1
            for pair in range(M_TILES // 2):
                score_banks[q, pair] = new_bank()
                score_pass(q, pair, 0, 0, E_COLS, True, False)
                score_pass(q, pair, 1, 0, J if is_last else E_COLS, False, not is_last)
            if is_last:
                for pair in range(M_TILES // 2):
                    score_pass(q, pair, 1, J, J, False, True)

        first_banks = [new_bank() for chunk in range(J_CHUNKS)]
        for a in range(K_PASSES - 1):
            for chunk in range(J_CHUNKS):
                x_pass(first_banks[chunk], 0, chunk, a)

        runs = [(b, chunk, 2) for b in range(R_HALVES) for chunk in range(0, J_CHUNKS, 2)]
        runs = [(0, 0, 1), (0, 1, 1)] + runs[1:-1] + [(R_HALVES - 1, J_CHUNKS - 2, 1), (R_HALVES - 1, J_CHUNKS - 1, 1)]
        side_work = [
            lambda: round_wb(1, 0, nc.vector.tensor_copy),
            lambda: (quantize_wb(1, 0), round_wb(1, 1, nc.vector.tensor_copy)),
            lambda: quantize_wb(1, 1),
            gather_v2_scales,
            lambda: gather_v2(0),
            lambda: gather_v2(1),
        ] + [lambda q=q: make_scores(q) for q in range(E_CHUNKS)]

        magnitudes, h_tiles = {}, {}
        for step in range(len(runs) + 2):
            if step < len(runs):
                b, first, count = runs[step]
                magnitudes[step] = ring.tile([P, E_COLS, PACK], F32, name="magnitude", bufs=2)
                for chunk in range(first, first + count):
                    if b == 0:
                        bank = first_banks[chunk]
                        x_pass(bank, b, chunk, K_PASSES - 1)
                    else:
                        bank = new_bank()
                        for a in range(K_PASSES):
                            x_pass(bank, b, chunk, a)
                    take_abs(bank, magnitudes[step][:, (chunk - first) * J : (chunk - first + 1) * J, :])
            if 1 <= step <= len(runs):
                b, first, count = runs[step - 1]
                h_tiles[step - 1] = apply_gain(take_root(magnitudes[step - 1], count * J), b, count * J)
            if step >= 2:
                b, first, count = runs[step - 2]
                quantize_h(b, first, count * J, h_tiles[step - 2])
                side_work[step - 2]()

        for m in range(M_TILES):
            pair, side = divmod(m, 2)
            for q in range(E_CHUNKS):
                copy = nc.vector.tensor_copy if (m == 0 and q == E_CHUNKS - 1) else nc.scalar.copy
                copy(scores[m][:, q * E_COLS : (q + 1) * E_COLS], score_banks[q, pair][:, side * E_COLS : (side + 1) * E_COLS])

        entry = [kept([P, PAIRS], F32, f"entry{m}") for m in range(M_TILES)]
        turns, sines = {}, {}

        def pick_entry(m):
            nc.vector.tensor_copy(entry[m][:], scores[m][:].indirect(p1[:]))

        def count_turns(m):
            turns[m] = ring.tile([P, PAIRS], I32, name="turns", bufs=2)
            nc.vector.tensor_scalar(turns[m][:], entry[m][:], 1.0 / (2.0 * math.pi), None, ALU.mult)

        def take_sine(m):
            angle = ring.tile([P, PAIRS], F32, name="angle", bufs=2)
            nc.vector.scalar_tensor_tensor(angle[:], turns[m][:], -2.0 * math.pi, entry[m][:], ALU.mult, ALU.add)
            sines[m] = ring.tile([P, PAIRS], F32, name="sine")
            nc.scalar.activation(sines[m][:], angle[:], ACT.Sin)

        def finish(m, first, width):
            cols = slice(first, first + width)
            product = ring.tile([P, PAIRS], F32, name="product", bufs=2)
            exits = scores[m][:].indirect(p2[:, first // PER_COLUMN : (first + width) // PER_COLUMN])
            nc.vector.tensor_tensor(product[:, :width], exits, sines[m][:, cols], ALU.mult)
            result = ring.tile([P, PAIRS], F32, name="result", bufs=M_TILES + 1)
            nc.scalar.activation(result[:, :width], product[:, :width], ACT.Identity, bias=defect_sb[:, m : m + 1], scale=-1.0)
            nc.sync.dma_start(out=out[m * P : (m + 1) * P, cols], in_=result[:, :width])

        pick_entry(0)
        pick_entry(1)
        for m in range(M_TILES):
            count_turns(m)
            if m + 2 < M_TILES:
                pick_entry(m + 2)
            else:
                finish(m - 2, 0, PAIRS)
            take_sine(m)
        finish(M_TILES - 2, 0, PAIRS)
        finish(M_TILES - 1, 0, PAIRS - LAST_PIECE)
        finish(M_TILES - 1, PAIRS - LAST_PIECE, LAST_PIECE)
